import numpy as np
import ml_dtypes


def mxq(x, axis, fmt="e4m3"):
    dtype, down = {"e4m3": (ml_dtypes.float8_e4m3fn, 7), "e5m2": (ml_dtypes.float8_e5m2, 14)}[fmt]
    v = np.moveaxis(np.asarray(x, np.float32).astype(ml_dtypes.bfloat16).astype(np.float64), axis, -1)
    blocks = v.reshape(v.shape[:-1] + (-1, 32))
    amax = np.abs(blocks).max(-1, keepdims=True)
    byte = np.maximum(np.where(amax > 0, np.frexp(amax)[1] - 1 + 127, 0) - down, 1)
    scale = np.exp2(byte - 127.0)
    codes = (blocks / scale).astype(np.float32).astype(dtype).astype(np.float64)
    return np.moveaxis((codes * scale).reshape(v.shape), -1, axis)


WIDE = False


def mx_kscale(k):
    if not WIDE:
        return np.ones(k)
    levels = np.array([10, -10, 5, -5, 0])
    if k % 512:
        return np.exp2(np.random.permutation(np.resize(levels, k // 32))).repeat(32)
    a = np.empty((k // 512, 16))
    for p in range(k // 512):
        a[p, :8] = np.random.permutation(np.resize(levels, 8))
        for g in range(8):
            far = levels[np.abs(levels - a[p, g]) >= 10]
            a[p, g + 8] = far[np.random.randint(len(far))]
    return np.exp2(a.ravel()).repeat(32)


def f64(x):
    return np.asarray(x).astype(np.float64)


def striped(idx):
    return np.tile(idx.reshape(-1, 16).T, (8, 1)).astype(np.uint16)


def unstriped(offs):
    return offs[:16].T.reshape(-1).astype(np.int64)


def pack_weight(w):
    k, n = w.shape
    w = f64(np.asarray(w, np.float32).astype(ml_dtypes.bfloat16)).reshape(k // 32, 32, n)
    amax = np.abs(w).max(1)
    byte = np.clip(np.where(amax > 0, np.frexp(amax)[1] - 1 + 127 - 7, 1), 1, 254)
    scaled = (w * np.exp2(127.0 - byte)[:, None, :]).reshape(k, n).astype(np.float32)
    words = np.ascontiguousarray(scaled.reshape(k // 512, 128, 4, n).transpose(0, 1, 3, 2)).astype(ml_dtypes.float8_e4m3fn).view(np.uint8)
    return words, np.ascontiguousarray(byte.astype(np.uint8).reshape(k // 512, 16, n))


def unpack_weight(words, scales):
    g, p, n, _ = words.shape
    vals = np.ascontiguousarray(words).view(ml_dtypes.float8_e4m3fn).astype(np.float64) * np.repeat(np.exp2(scales.astype(np.float64) - 127.0), 8, axis=1)[..., None]
    return vals.transpose(0, 1, 3, 2).reshape(g * 512, n)


def relu2(v):
    return np.maximum(v, 0.0) ** 2


K, T, E, C, N = 1536, 1536, 4, 256, 128


def by_expert(wq, xq):
    return np.concatenate([wq[e].T @ xq[:, e * C:(e + 1) * C] for e in range(E)], axis=1)


def setup_inputs():
    n = np.random.standard_normal
    s = mx_kscale(K)[:, None]
    packed = [pack_weight(m) for m in n((E, K, N)) / np.sqrt(K) / s[None]]
    return {
        "xT": (n((K, T)) * s).astype(np.float32),
        "xr": n((N, T)).astype(np.float32),
        "w_words": np.stack([m[0] for m in packed]),
        "w_scales": np.stack([m[1] for m in packed]),
        "b": (0.3 * n((N, E))).astype(np.float32),
        "gate": np.tile(np.random.uniform(0.2, 1.0, E * C), (N, 1)).astype(np.float32),
        "offs": striped(np.random.permutation(T)[:E * C]),
    }


def reference(xT, xr, w_words, w_scales, b, gate, offs):
    idx = unstriped(offs)
    w = np.stack([unpack_weight(w_words[e], w_scales[e]) for e in range(E)])
    xq = mxq(f64(xT)[:, idx], 0, "e4m3")
    y = by_expert(w, xq)
    y = relu2(y + np.repeat(f64(b), C, axis=1))
    out = f64(xr).copy()
    out[:, idx] += f64(gate) * y
    return out

@@ -1,0 +1,143 @@
+from contextlib import ExitStack
+
+import concourse.mybir as mybir
+
+K, T, E, C, N = 1536, 1536, 4, 256, 128
+SLOTS = E * C
+P = 128
+PACK = 4
+PASSES = K // (P * PACK)
+FLOPS = 2 * K * N * SLOTS
+
+F32 = mybir.dt.float32
+BF16 = mybir.dt.bfloat16
+I32 = mybir.dt.int32
+U32 = mybir.dt.uint32
+U16 = mybir.dt.uint16
+U8 = mybir.dt.uint8
+FP8X4 = mybir.dt.float8_e4m3fn_x4
+Act = mybir.ActivationFunctionType
+Alu = mybir.AluOpType
+
+CHUNKS = (
+    ((256, 96), (256, 96), (512, 192), (512, 192)),
+    ((512, 192), (512, 192), (512, 192)),
+    ((512, 192), (512, 192), (256, 128), (256, 160)),
+)
+
+
+def interleave(tile, c0, c1):
+    return tile[:, c0:c1, :].rearrange("p (c i) t -> p c t i", i=4)
+
+
+def deinterleave(tile, c0, c1):
+    return tile[:, :, c0:c1].rearrange("p t (c i) -> p c t i", i=4)
+
+
+def tile_moe_res_lin_relu2_kernel(tc, xT, xr, w_words, w_scales, b, gate, offs, out):
+    nc = tc.nc
+    with ExitStack() as ctx:
+        keep = ctx.enter_context(tc.tile_pool(name="keep", bufs=1))
+        psum = ctx.enter_context(tc.psum_pool(name="psum", bufs=1))
+
+        offsets = keep.tile([P, SLOTS // 16], U16, name="offsets")
+        w_codes = keep.tile([P, E * PASSES, N], U32, name="w_codes", align_bytes=64)
+        w_scale = keep.tile([P, E * PASSES, N], U8, name="w_scale", align_bytes=64)
+        bias = keep.tile([P, E], F32, name="bias")
+        gates = keep.tile([P, SLOTS], F32, name="gates")
+        resid = keep.tile([P, T], F32, name="resid")
+        window = keep.tile([P, T], F32, name="window")
+        total = keep.tile([P, T], F32, name="total")
+        plane = keep.tile([P, T], U8, name="plane", align_bytes=64)
+        slot_plane = keep.tile([P, SLOTS], U8, name="slot_plane", align_bytes=64)
+        warm = keep.tile([P, 8], F32, name="warm")
+        warmed = keep.tile([P, 8], F32, name="warmed")
+        codes = [keep.tile([P, T], U32, name=f"codes{a}", align_bytes=64) for a in range(PASSES)]
+        slot_codes = [keep.tile([P, SLOTS], U32, name=f"slot_codes{a}", align_bytes=64) for a in range(PASSES)]
+
+        nc.vector.memset(warm[:], 0.0)
+        nc.scalar.activation(warmed[:], warm[:], Act.Relu)
+        nc.gpsimd.memset(plane[:], 0)
+        nc.vector.memset(w_scale[:].rearrange("p g n -> p (g n)").bitcast(I32), 0)
+        nc.vector.memset(window[:], 0.0)
+
+        raws = {}
+        for a in range(PASSES):
+            rows = xT[a * P * PACK : (a + 1) * P * PACK, :].rearrange("(p r) t -> p r t", r=PACK)
+            t0 = 0
+            for i, (width, v) in enumerate(CHUNKS[a]):
+                raws[a, i] = keep.tile([P, PACK, width], F32, name=f"raw{a}_{i}")
+                nc.sync.dma_start(out=raws[a, i][:], in_=rows[:, :, t0 : t0 + width])
+                t0 += width
+                if a == 0 and i == 0:
+                    nc.sync.dma_start(offsets[:], offs)
+        nc.sync.dma_start(
+            out=w_codes[:].rearrange("p g n -> p (g n)").bitcast(I32),
+            in_=w_words.rearrange("e a p n r -> p (e a) (n r)").bitcast(I32),
+        )
+        for q in range(4):
+            nc.sync.dma_start(
+                out=w_scale[32 * q : 32 * q + 4, :, :].bitcast(I32),
+                in_=w_scales[:, :, 4 * q : 4 * q + 4, :].rearrange("e a r n -> r (e a) n").bitcast(I32),
+            )
+        nc.sync.dma_start(out=bias[:], in_=b)
+        nc.sync.dma_start(out=gates[:], in_=gate)
+        nc.sync.dma_start(out=resid[:], in_=xr)
+
+        def round_chunk(a, i, width, v):
+            packed = keep.tile([P, width, PACK], BF16, name=f"bf{a}_{i}", align_bytes=64)
+            raw = raws[a, i]
+            if v > 0:
+                nc.vector.tensor_copy(out=interleave(packed, 0, v), in_=deinterleave(raw, 0, v))
+            if v < width:
+                nc.scalar.activation(interleave(packed, v, width), deinterleave(raw, v, width), Act.Copy)
+            return packed
+
+        def quantise(a, t0, width, packed):
+            nc.vector.quantize_mx(
+                out=codes[a][:, t0 : t0 + width].bitcast(FP8X4),
+                scales=plane[4 * a : P, t0 : t0 + width],
+                in_=packed[:].rearrange("p c t -> p (c t)"),
+            )
+
+        def gather_words(a):
+            nc.vector.tensor_copy(out=slot_codes[a][:], in_=codes[a][:].indirect(offsets[:]))
+
+        for a in range(PASSES):
+            t0 = 0
+            for i, (width, v) in enumerate(CHUNKS[a]):
+                packed = round_chunk(a, i, width, v)
+                quantise(a, t0, width, packed)
+                t0 += width
+            gather_words(a)
+
+        sums = []
+        for e in range(E):
+            cols = slice(e * C, (e + 1) * C)
+            nc.vector.tensor_copy(out=slot_plane[:, cols], in_=plane[:].indirect(offsets[:, e * (C // 16) : (e + 1) * (C // 16)]))
+            acc = psum.tile([P, C], F32, name=f"acc{e}")
+            for a in range(PASSES):
+                nc.tensor.matmul_mx(
+                    out=acc[:],
+                    lhsT=w_codes[:, e * PASSES + a, :].bitcast(FP8X4),
+                    lhsT_scale=w_scale[:, e * PASSES + a, :],
+                    rhs=slot_codes[a][:, cols].bitcast(FP8X4),
+                    rhs_scale=slot_plane[4 * a : P, cols],
+                    start=(a == 0),
+                    stop=(a == PASSES - 1),
+                )
+            relu = keep.tile([P, C], F32, name=f"relu{e}")
+            nc.scalar.activation(relu[:], acc[:], Act.Relu, bias=bias[:, e : e + 1])
+            square = keep.tile([P, C], F32, name=f"square{e}")
+            nc.scalar.activation(square[:], relu[:], Act.Square)
+            sums.append(square)
+        for e in range(E):
+            cols = slice(e * C, (e + 1) * C)
+            where = offsets[:, e * (C // 16) : (e + 1) * (C // 16)]
+            gated = keep.tile([P, C], F32, name=f"gated{e}")
+            nc.vector.tensor_tensor(gated[:], sums[e][:], gates[:, cols], Alu.mult)
+            nc.vector.tensor_copy(out=window[:].indirect(where), in_=gated[:])
+        for t0 in range(0, T, 512):
+            cols = slice(t0, t0 + 512)
+            nc.vector.tensor_tensor(total[:, cols], window[:, cols], resid[:, cols], Alu.add)
+            nc.sync.dma_start(out=out[:, cols], in_=total[:, cols])

@@ -20,10 +20,12 @@ Act = mybir.ActivationFunctionType
 Alu = mybir.AluOpType
 
 CHUNKS = (
-    ((256, 96), (256, 96), (512, 192), (512, 192)),
-    ((512, 192), (512, 192), (512, 192)),
-    ((512, 192), (512, 192), (256, 128), (256, 160)),
+    ((256, 96), (256, 96), (512, 160), (512, 256)),
+    ((512, 128), (512, 128), (256, 128), (256, 160)),
+    ((512, 96), (512, 160), (256, 96), (256, 160)),
 )
+
+SCATTERS = ((0, 512), (512, 512))
 
 
 def interleave(tile, c0, c1):
@@ -100,8 +102,9 @@ def tile_moe_res_lin_relu2_kernel(tc, xT, xr, w_words, w_scales, b, gate, offs, 
                 in_=packed[:].rearrange("p c t -> p (c t)"),
             )
 
-        def gather_words(a):
-            nc.vector.tensor_copy(out=slot_codes[a][:], in_=codes[a][:].indirect(offsets[:]))
+        def gather(window_tile, result, j0, width):
+            where = offsets[:, j0 // 16 : (j0 + width) // 16]
+            nc.vector.tensor_copy(out=result[:, j0 : j0 + width], in_=window_tile[:].indirect(where))
 
         for a in range(PASSES):
             t0 = 0
@@ -109,35 +112,36 @@ def tile_moe_res_lin_relu2_kernel(tc, xT, xr, w_words, w_scales, b, gate, offs, 
                 packed = round_chunk(a, i, width, v)
                 quantise(a, t0, width, packed)
                 t0 += width
-            gather_words(a)
+            if a < PASSES - 1:
+                for j0 in range(0, SLOTS, 1024):
+                    gather(codes[a], slot_codes[a], j0, 1024)
 
-        sums = []
-        for e in range(E):
-            cols = slice(e * C, (e + 1) * C)
-            nc.vector.tensor_copy(out=slot_plane[:, cols], in_=plane[:].indirect(offsets[:, e * (C // 16) : (e + 1) * (C // 16)]))
-            acc = psum.tile([P, C], F32, name=f"acc{e}")
-            for a in range(PASSES):
-                nc.tensor.matmul_mx(
-                    out=acc[:],
-                    lhsT=w_codes[:, e * PASSES + a, :].bitcast(FP8X4),
-                    lhsT_scale=w_scale[:, e * PASSES + a, :],
-                    rhs=slot_codes[a][:, cols].bitcast(FP8X4),
-                    rhs_scale=slot_plane[4 * a : P, cols],
-                    start=(a == 0),
-                    stop=(a == PASSES - 1),
-                )
-            relu = keep.tile([P, C], F32, name=f"relu{e}")
-            nc.scalar.activation(relu[:], acc[:], Act.Relu, bias=bias[:, e : e + 1])
-            square = keep.tile([P, C], F32, name=f"square{e}")
-            nc.scalar.activation(square[:], relu[:], Act.Square)
-            sums.append(square)
-        for e in range(E):
-            cols = slice(e * C, (e + 1) * C)
-            where = offsets[:, e * (C // 16) : (e + 1) * (C // 16)]
-            gated = keep.tile([P, C], F32, name=f"gated{e}")
-            nc.vector.tensor_tensor(gated[:], sums[e][:], gates[:, cols], Alu.mult)
-            nc.vector.tensor_copy(out=window[:].indirect(where), in_=gated[:])
-        for t0 in range(0, T, 512):
-            cols = slice(t0, t0 + 512)
+        relu = keep.tile([P, SLOTS], F32, name="relu")
+        square = keep.tile([P, SLOTS], F32, name="square")
+        for j0 in range(0, SLOTS, 512):
+            gather(codes[PASSES - 1], slot_codes[PASSES - 1], j0, 512)
+            for j1 in range(j0, j0 + 512, 512):
+                gather(plane, slot_plane, j1, 512)
+            for e in range(j0 // C, (j0 + 512) // C):
+                cols = slice(e * C, (e + 1) * C)
+                acc = psum.tile([P, C], F32, name=f"acc{e}")
+                for a in range(PASSES):
+                    nc.tensor.matmul_mx(
+                        out=acc[:],
+                        lhsT=w_codes[:, e * PASSES + a, :].bitcast(FP8X4),
+                        lhsT_scale=w_scale[:, e * PASSES + a, :],
+                        rhs=slot_codes[a][:, cols].bitcast(FP8X4),
+                        rhs_scale=slot_plane[4 * a : P, cols],
+                        start=(a == 0),
+                        stop=(a == PASSES - 1),
+                    )
+                nc.scalar.activation(relu[:, cols], acc[:], Act.Relu, bias=bias[:, e : e + 1])
+                nc.scalar.activation(square[:, cols], relu[:, cols], Act.Square)
+        for j0, width in SCATTERS:
+            cols = slice(j0, j0 + width)
+            where = offsets[:, j0 // 16 : (j0 + width) // 16]
+            nc.vector.tensor_tensor(window[:].indirect(where), square[:, cols], gates[:, cols], Alu.mult)
+        for t0, width in ((0, 640), (640, 512), (1152, 384)):
+            cols = slice(t0, t0 + width)
             nc.vector.tensor_tensor(total[:, cols], window[:, cols], resid[:, cols], Alu.add)
             nc.sync.dma_start(out=out[:, cols], in_=total[:, cols])

@@ -19,13 +19,14 @@ FP8X4 = mybir.dt.float8_e4m3fn_x4
 Act = mybir.ActivationFunctionType
 Alu = mybir.AluOpType
 
+LOADS = ((1024, 512), (1024, 512), (768, 512, 256))
 CHUNKS = (
-    ((256, 96), (256, 96), (512, 160), (512, 256)),
+    ((512, 176), (512, 176), (512, 208)),
     ((512, 128), (512, 128), (256, 128), (256, 160)),
-    ((512, 96), (512, 160), (256, 96), (256, 160)),
+    ((512, 96), (256, 64), (512, 160), (256, 160)),
 )
 
-SCATTERS = ((0, 512), (512, 512))
+SCATTERS = ((0, 256), (256, 256), (512, 256), (768, 256))
 
 
 def interleave(tile, c0, c1):
@@ -67,9 +68,10 @@ def tile_moe_res_lin_relu2_kernel(tc, xT, xr, w_words, w_scales, b, gate, offs, 
         for a in range(PASSES):
             rows = xT[a * P * PACK : (a + 1) * P * PACK, :].rearrange("(p r) t -> p r t", r=PACK)
             t0 = 0
-            for i, (width, v) in enumerate(CHUNKS[a]):
-                raws[a, i] = keep.tile([P, PACK, width], F32, name=f"raw{a}_{i}")
-                nc.sync.dma_start(out=raws[a, i][:], in_=rows[:, :, t0 : t0 + width])
+            for i, width in enumerate(LOADS[a]):
+                raw = keep.tile([P, PACK, width], F32, name=f"raw{a}_{i}")
+                nc.sync.dma_start(out=raw[:], in_=rows[:, :, t0 : t0 + width])
+                raws[a, t0] = raw
                 t0 += width
                 if a == 0 and i == 0:
                     nc.sync.dma_start(offsets[:], offs)
@@ -86,13 +88,14 @@ def tile_moe_res_lin_relu2_kernel(tc, xT, xr, w_words, w_scales, b, gate, offs, 
         nc.sync.dma_start(out=gates[:], in_=gate)
         nc.sync.dma_start(out=resid[:], in_=xr)
 
-        def round_chunk(a, i, width, v):
-            packed = keep.tile([P, width, PACK], BF16, name=f"bf{a}_{i}", align_bytes=64)
-            raw = raws[a, i]
+        def round_chunk(a, t0, width, v):
+            packed = keep.tile([P, width, PACK], BF16, name=f"bf{a}_{t0}", align_bytes=64)
+            start = max(s for (p, s) in raws if p == a and s <= t0)
+            raw, c = raws[a, start], t0 - start
             if v > 0:
-                nc.vector.tensor_copy(out=interleave(packed, 0, v), in_=deinterleave(raw, 0, v))
+                nc.vector.tensor_copy(out=interleave(packed, 0, v), in_=deinterleave(raw, c, c + v))
             if v < width:
-                nc.scalar.activation(interleave(packed, v, width), deinterleave(raw, v, width), Act.Copy)
+                nc.scalar.activation(interleave(packed, v, width), deinterleave(raw, c + v, c + width), Act.Copy)
             return packed
 
         def quantise(a, t0, width, packed):
@@ -108,8 +111,8 @@ def tile_moe_res_lin_relu2_kernel(tc, xT, xr, w_words, w_scales, b, gate, offs, 
 
         for a in range(PASSES):
             t0 = 0
-            for i, (width, v) in enumerate(CHUNKS[a]):
-                packed = round_chunk(a, i, width, v)
+            for width, v in CHUNKS[a]:
+                packed = round_chunk(a, t0, width, v)
                 quantise(a, t0, width, packed)
                 t0 += width
             if a < PASSES - 1:

@@ -21,9 +21,9 @@ Alu = mybir.AluOpType
 
 LOADS = ((1024, 512), (1024, 512), (768, 512, 256))
 CHUNKS = (
-    ((512, 176), (512, 176), (512, 208)),
-    ((512, 128), (512, 128), (256, 128), (256, 160)),
-    ((512, 96), (256, 64), (512, 160), (256, 160)),
+    ((512, 304), (512, 336), (512, 288)),
+    ((512, 288), (512, 304), (512, 336)),
+    ((512, 256), (256, 96), (512, 272), (256, 160)),
 )
 
 SCATTERS = ((0, 256), (256, 256), (512, 256), (768, 256))
@@ -75,16 +75,18 @@ def tile_moe_res_lin_relu2_kernel(tc, xT, xr, w_words, w_scales, b, gate, offs, 
                 t0 += width
                 if a == 0 and i == 0:
                     nc.sync.dma_start(offsets[:], offs)
-        nc.sync.dma_start(
-            out=w_codes[:].rearrange("p g n -> p (g n)").bitcast(I32),
-            in_=w_words.rearrange("e a p n r -> p (e a) (n r)").bitcast(I32),
-        )
         for q in range(4):
             nc.sync.dma_start(
                 out=w_scale[32 * q : 32 * q + 4, :, :].bitcast(I32),
                 in_=w_scales[:, :, 4 * q : 4 * q + 4, :].rearrange("e a r n -> r (e a) n").bitcast(I32),
             )
-        nc.sync.dma_start(out=bias[:], in_=b)
+        for e in range(0, E, 2):
+            nc.sync.dma_start(
+                out=w_codes[:, e * PASSES : (e + 2) * PASSES, :].rearrange("p g n -> p (g n)").bitcast(I32),
+                in_=w_words[e : e + 2].rearrange("e a p n r -> p (e a) (n r)").bitcast(I32),
+            )
+            if e == 0:
+                nc.sync.dma_start(out=bias[:], in_=b)
         nc.sync.dma_start(out=gates[:], in_=gate)
         nc.sync.dma_start(out=resid[:], in_=xr)
 
@@ -144,7 +146,7 @@ def tile_moe_res_lin_relu2_kernel(tc, xT, xr, w_words, w_scales, b, gate, offs, 
             cols = slice(j0, j0 + width)
             where = offsets[:, j0 // 16 : (j0 + width) // 16]
             nc.vector.tensor_tensor(window[:].indirect(where), square[:, cols], gates[:, cols], Alu.mult)
-        for t0, width in ((0, 640), (640, 512), (1152, 384)):
+        for t0, width in ((0, 768), (768, 512), (1280, 256)):
             cols = slice(t0, t0 + width)
             nc.vector.tensor_tensor(total[:, cols], window[:, cols], resid[:, cols], Alu.add)
             nc.sync.dma_start(out=out[:, cols], in_=total[:, cols])

@@ -7,6 +7,8 @@ SLOTS = E * C
 P = 128
 PACK = 4
 PASSES = K // (P * PACK)
+OFFSETS_PER_COLUMN = 16
+
 FLOPS = 2 * K * N * SLOTS
 
 F32 = mybir.dt.float32
@@ -20,21 +22,23 @@ Act = mybir.ActivationFunctionType
 Alu = mybir.AluOpType
 
 LOADS = ((1024, 512), (1024, 512), (768, 512, 256))
+
 CHUNKS = (
-    ((512, 304), (512, 336), (512, 288)),
-    ((512, 288), (512, 304), (512, 336)),
-    ((512, 256), (256, 96), (512, 272), (256, 160)),
+    ((512, 320), (512, 336), (512, 256)),
+    ((512, 272), (512, 288), (512, 320)),
+    ((512, 272), (256, 96), (512, 240), (256, 192)),
 )
 
-SCATTERS = ((0, 256), (256, 256), (512, 256), (768, 256))
+LAST_GATHERS = (
+    ((0, 512), ((0, 256), (256, 256))),
+    ((512, 512), ((512, 512),)),
+)
 
+SCATTERS = ((0, 512), (512, 512))
 
-def interleave(tile, c0, c1):
-    return tile[:, c0:c1, :].rearrange("p (c i) t -> p c t i", i=4)
+STORES = ((0, 640), (640, 640), (1280, 256))
 
-
-def deinterleave(tile, c0, c1):
-    return tile[:, :, c0:c1].rearrange("p t (c i) -> p c t i", i=4)
+RUN = 4
 
 
 def tile_moe_res_lin_relu2_kernel(tc, xT, xr, w_words, w_scales, b, gate, offs, out):
@@ -43,42 +47,44 @@ def tile_moe_res_lin_relu2_kernel(tc, xT, xr, w_words, w_scales, b, gate, offs, 
         keep = ctx.enter_context(tc.tile_pool(name="keep", bufs=1))
         psum = ctx.enter_context(tc.psum_pool(name="psum", bufs=1))
 
-        offsets = keep.tile([P, SLOTS // 16], U16, name="offsets")
+        offsets = keep.tile([P, SLOTS // OFFSETS_PER_COLUMN], U16, name="offsets")
         w_codes = keep.tile([P, E * PASSES, N], U32, name="w_codes", align_bytes=64)
-        w_scale = keep.tile([P, E * PASSES, N], U8, name="w_scale", align_bytes=64)
+        w_bytes = keep.tile([P, E * PASSES, N], U8, name="w_bytes", align_bytes=64)
         bias = keep.tile([P, E], F32, name="bias")
         gates = keep.tile([P, SLOTS], F32, name="gates")
         resid = keep.tile([P, T], F32, name="resid")
         window = keep.tile([P, T], F32, name="window")
         total = keep.tile([P, T], F32, name="total")
-        plane = keep.tile([P, T], U8, name="plane", align_bytes=64)
-        slot_plane = keep.tile([P, SLOTS], U8, name="slot_plane", align_bytes=64)
-        warm = keep.tile([P, 8], F32, name="warm")
-        warmed = keep.tile([P, 8], F32, name="warmed")
-        codes = [keep.tile([P, T], U32, name=f"codes{a}", align_bytes=64) for a in range(PASSES)]
+        token_codes = [keep.tile([P, T], U32, name=f"token_codes{a}", align_bytes=64) for a in range(PASSES)]
+        token_bytes = keep.tile([P, T], U8, name="token_bytes", align_bytes=64)
         slot_codes = [keep.tile([P, SLOTS], U32, name=f"slot_codes{a}", align_bytes=64) for a in range(PASSES)]
+        slot_bytes = keep.tile([P, SLOTS], U8, name="slot_bytes", align_bytes=64)
+        relu = keep.tile([P, SLOTS], F32, name="relu")
+        square = keep.tile([P, SLOTS], F32, name="square")
+        zeros = keep.tile([P, 8], F32, name="zeros")
+        table_load = keep.tile([P, 8], F32, name="table_load")
 
-        nc.vector.memset(warm[:], 0.0)
-        nc.scalar.activation(warmed[:], warm[:], Act.Relu)
-        nc.gpsimd.memset(plane[:], 0)
-        nc.vector.memset(w_scale[:].rearrange("p g n -> p (g n)").bitcast(I32), 0)
+        nc.vector.memset(zeros[:], 0.0)
+        nc.scalar.activation(table_load[:], zeros[:], Act.Relu)
+        nc.gpsimd.memset(token_bytes[:], 0)
+        nc.vector.memset(w_bytes[:].rearrange("p g n -> p (g n)").bitcast(I32), 0)
         nc.vector.memset(window[:], 0.0)
 
         raws = {}
         for a in range(PASSES):
             rows = xT[a * P * PACK : (a + 1) * P * PACK, :].rearrange("(p r) t -> p r t", r=PACK)
             t0 = 0
-            for i, width in enumerate(LOADS[a]):
-                raw = keep.tile([P, PACK, width], F32, name=f"raw{a}_{i}")
+            for width in LOADS[a]:
+                raw = keep.tile([P, PACK, width], F32, name=f"raw{a}_{t0}")
                 nc.sync.dma_start(out=raw[:], in_=rows[:, :, t0 : t0 + width])
+                if not raws:
+                    nc.sync.dma_start(offsets[:], offs)
                 raws[a, t0] = raw
                 t0 += width
-                if a == 0 and i == 0:
-                    nc.sync.dma_start(offsets[:], offs)
-        for q in range(4):
+        for quadrant in range(4):
             nc.sync.dma_start(
-                out=w_scale[32 * q : 32 * q + 4, :, :].bitcast(I32),
-                in_=w_scales[:, :, 4 * q : 4 * q + 4, :].rearrange("e a r n -> r (e a) n").bitcast(I32),
+                out=w_bytes[32 * quadrant : 32 * quadrant + 4, :, :].bitcast(I32),
+                in_=w_scales[:, :, 4 * quadrant : 4 * quadrant + 4, :].rearrange("e a q n -> q (e a) n").bitcast(I32),
             )
         for e in range(0, E, 2):
             nc.sync.dma_start(
@@ -90,63 +96,69 @@ def tile_moe_res_lin_relu2_kernel(tc, xT, xr, w_words, w_scales, b, gate, offs, 
         nc.sync.dma_start(out=gates[:], in_=gate)
         nc.sync.dma_start(out=resid[:], in_=xr)
 
-        def round_chunk(a, t0, width, v):
-            packed = keep.tile([P, width, PACK], BF16, name=f"bf{a}_{t0}", align_bytes=64)
-            start = max(s for (p, s) in raws if p == a and s <= t0)
-            raw, c = raws[a, start], t0 - start
-            if v > 0:
-                nc.vector.tensor_copy(out=interleave(packed, 0, v), in_=deinterleave(raw, c, c + v))
-            if v < width:
-                nc.scalar.activation(interleave(packed, v, width), deinterleave(raw, c + v, c + width), Act.Copy)
-            return packed
+        def by_runs(raw, t0, t1):
+            return raw[:, :, t0:t1].rearrange("p r (c i) -> p c r i", i=RUN)
 
-        def quantise(a, t0, width, packed):
+        def interleaved(packed, t0, t1):
+            return packed[:, t0:t1, :].rearrange("p (c i) r -> p c r i", i=RUN)
+
+        def round_and_quantise(a, t0, width, by_vector):
+            load0 = max(start for pass_, start in raws if pass_ == a and start <= t0)
+            raw, c0 = raws[a, load0], t0 - load0
+            packed = keep.tile([P, width, PACK], BF16, name=f"packed{a}_{t0}", align_bytes=64)
+            nc.vector.tensor_copy(out=interleaved(packed, 0, by_vector), in_=by_runs(raw, c0, c0 + by_vector))
+            nc.scalar.activation(
+                interleaved(packed, by_vector, width), by_runs(raw, c0 + by_vector, c0 + width), Act.Copy
+            )
             nc.vector.quantize_mx(
-                out=codes[a][:, t0 : t0 + width].bitcast(FP8X4),
-                scales=plane[4 * a : P, t0 : t0 + width],
-                in_=packed[:].rearrange("p c t -> p (c t)"),
+                out=token_codes[a][:, t0 : t0 + width].bitcast(FP8X4),
+                scales=token_bytes[4 * a : P, t0 : t0 + width],
+                in_=packed[:].rearrange("p t r -> p (t r)"),
             )
 
-        def gather(window_tile, result, j0, width):
-            where = offsets[:, j0 // 16 : (j0 + width) // 16]
-            nc.vector.tensor_copy(out=result[:, j0 : j0 + width], in_=window_tile[:].indirect(where))
+        def offsets_of(j0, slots):
+            return offsets[:, j0 // OFFSETS_PER_COLUMN : (j0 + slots) // OFFSETS_PER_COLUMN]
+
+        def gather(of_slots, of_tokens, j0, slots):
+            nc.vector.tensor_copy(out=of_slots[:, j0 : j0 + slots], in_=of_tokens[:].indirect(offsets_of(j0, slots)))
+
+        def expert(e):
+            slots = slice(e * C, (e + 1) * C)
+            acc = psum.tile([P, C], F32, name=f"acc{e}")
+            for a in range(PASSES):
+                nc.tensor.matmul_mx(
+                    out=acc[:],
+                    lhsT=w_codes[:, e * PASSES + a, :].bitcast(FP8X4),
+                    lhsT_scale=w_bytes[:, e * PASSES + a, :],
+                    rhs=slot_codes[a][:, slots].bitcast(FP8X4),
+                    rhs_scale=slot_bytes[4 * a : P, slots],
+                    start=(a == 0),
+                    stop=(a == PASSES - 1),
+                )
+            nc.scalar.activation(relu[:, slots], acc[:], Act.Relu, bias=bias[:, e : e + 1])
+            nc.scalar.activation(square[:, slots], relu[:, slots], Act.Square)
 
         for a in range(PASSES):
             t0 = 0
-            for width, v in CHUNKS[a]:
-                packed = round_chunk(a, t0, width, v)
-                quantise(a, t0, width, packed)
+            for width, by_vector in CHUNKS[a]:
+                round_and_quantise(a, t0, width, by_vector)
                 t0 += width
             if a < PASSES - 1:
-                for j0 in range(0, SLOTS, 1024):
-                    gather(codes[a], slot_codes[a], j0, 1024)
+                gather(slot_codes[a], token_codes[a], 0, SLOTS)
 
-        relu = keep.tile([P, SLOTS], F32, name="relu")
-        square = keep.tile([P, SLOTS], F32, name="square")
-        for j0 in range(0, SLOTS, 512):
-            gather(codes[PASSES - 1], slot_codes[PASSES - 1], j0, 512)
-            for j1 in range(j0, j0 + 512, 512):
-                gather(plane, slot_plane, j1, 512)
-            for e in range(j0 // C, (j0 + 512) // C):
-                cols = slice(e * C, (e + 1) * C)
-                acc = psum.tile([P, C], F32, name=f"acc{e}")
-                for a in range(PASSES):
-                    nc.tensor.matmul_mx(
-                        out=acc[:],
-                        lhsT=w_codes[:, e * PASSES + a, :].bitcast(FP8X4),
-                        lhsT_scale=w_scale[:, e * PASSES + a, :],
-                        rhs=slot_codes[a][:, cols].bitcast(FP8X4),
-                        rhs_scale=slot_plane[4 * a : P, cols],
-                        start=(a == 0),
-                        stop=(a == PASSES - 1),
-                    )
-                nc.scalar.activation(relu[:, cols], acc[:], Act.Relu, bias=bias[:, e : e + 1])
-                nc.scalar.activation(square[:, cols], relu[:, cols], Act.Square)
-        for j0, width in SCATTERS:
-            cols = slice(j0, j0 + width)
-            where = offsets[:, j0 // 16 : (j0 + width) // 16]
-            nc.vector.tensor_tensor(window[:].indirect(where), square[:, cols], gates[:, cols], Alu.mult)
-        for t0, width in ((0, 768), (768, 512), (1280, 256)):
+        for (j0, slots), byte_gathers in LAST_GATHERS:
+            gather(slot_codes[PASSES - 1], token_codes[PASSES - 1], j0, slots)
+            for byte_j0, byte_slots in byte_gathers:
+                gather(slot_bytes, token_bytes, byte_j0, byte_slots)
+            for e in range(j0 // C, (j0 + slots) // C):
+                expert(e)
+
+        for j0, slots in SCATTERS:
+            cols = slice(j0, j0 + slots)
+            nc.vector.tensor_tensor(
+                window[:].indirect(offsets_of(j0, slots)), square[:, cols], gates[:, cols], Alu.mult
+            )
+        for t0, width in STORES:
             cols = slice(t0, t0 + width)
             nc.vector.tensor_tensor(total[:, cols], window[:, cols], resid[:, cols], Alu.add)
             nc.sync.dma_start(out=out[:, cols], in_=total[:, cols])

from contextlib import ExitStack

import concourse.mybir as mybir

K, T, E, C, N = 1536, 1536, 4, 256, 128
SLOTS = E * C
P = 128
PACK = 4
PASSES = K // (P * PACK)
OFFSETS_PER_COLUMN = 16

FLOPS = 2 * K * N * SLOTS

F32 = mybir.dt.float32
BF16 = mybir.dt.bfloat16
I32 = mybir.dt.int32
U32 = mybir.dt.uint32
U16 = mybir.dt.uint16
U8 = mybir.dt.uint8
FP8X4 = mybir.dt.float8_e4m3fn_x4
Act = mybir.ActivationFunctionType
Alu = mybir.AluOpType

LOADS = ((1024, 512), (1024, 512), (768, 512, 256))

CHUNKS = (
    ((512, 320), (512, 336), (512, 256)),
    ((512, 272), (512, 288), (512, 320)),
    ((512, 272), (256, 96), (512, 240), (256, 192)),
)

LAST_GATHERS = (
    ((0, 512), ((0, 256), (256, 256))),
    ((512, 512), ((512, 512),)),
)

SCATTERS = ((0, 512), (512, 512))

STORES = ((0, 640), (640, 640), (1280, 256))

RUN = 4


def tile_moe_res_lin_relu2_kernel(tc, xT, xr, w_words, w_scales, b, gate, offs, out):
    nc = tc.nc
    with ExitStack() as ctx:
        keep = ctx.enter_context(tc.tile_pool(name="keep", bufs=1))
        psum = ctx.enter_context(tc.psum_pool(name="psum", bufs=1))

        offsets = keep.tile([P, SLOTS // OFFSETS_PER_COLUMN], U16, name="offsets")
        w_codes = keep.tile([P, E * PASSES, N], U32, name="w_codes", align_bytes=64)
        w_bytes = keep.tile([P, E * PASSES, N], U8, name="w_bytes", align_bytes=64)
        bias = keep.tile([P, E], F32, name="bias")
        gates = keep.tile([P, SLOTS], F32, name="gates")
        resid = keep.tile([P, T], F32, name="resid")
        window = keep.tile([P, T], F32, name="window")
        total = keep.tile([P, T], F32, name="total")
        token_codes = [keep.tile([P, T], U32, name=f"token_codes{a}", align_bytes=64) for a in range(PASSES)]
        token_bytes = keep.tile([P, T], U8, name="token_bytes", align_bytes=64)
        slot_codes = [keep.tile([P, SLOTS], U32, name=f"slot_codes{a}", align_bytes=64) for a in range(PASSES)]
        slot_bytes = keep.tile([P, SLOTS], U8, name="slot_bytes", align_bytes=64)
        relu = keep.tile([P, SLOTS], F32, name="relu")
        square = keep.tile([P, SLOTS], F32, name="square")
        zeros = keep.tile([P, 8], F32, name="zeros")
        table_load = keep.tile([P, 8], F32, name="table_load")

        nc.vector.memset(zeros[:], 0.0)
        nc.scalar.activation(table_load[:], zeros[:], Act.Relu)
        nc.gpsimd.memset(token_bytes[:], 0)
        nc.vector.memset(w_bytes[:].rearrange("p g n -> p (g n)").bitcast(I32), 0)
        nc.vector.memset(window[:], 0.0)

        raws = {}
        for a in range(PASSES):
            rows = xT[a * P * PACK : (a + 1) * P * PACK, :].rearrange("(p r) t -> p r t", r=PACK)
            t0 = 0
            for width in LOADS[a]:
                raw = keep.tile([P, PACK, width], F32, name=f"raw{a}_{t0}")
                nc.sync.dma_start(out=raw[:], in_=rows[:, :, t0 : t0 + width])
                if not raws:
                    nc.sync.dma_start(offsets[:], offs)
                raws[a, t0] = raw
                t0 += width
        for quadrant in range(4):
            nc.sync.dma_start(
                out=w_bytes[32 * quadrant : 32 * quadrant + 4, :, :].bitcast(I32),
                in_=w_scales[:, :, 4 * quadrant : 4 * quadrant + 4, :].rearrange("e a q n -> q (e a) n").bitcast(I32),
            )
        for e in range(0, E, 2):
            nc.sync.dma_start(
                out=w_codes[:, e * PASSES : (e + 2) * PASSES, :].rearrange("p g n -> p (g n)").bitcast(I32),
                in_=w_words[e : e + 2].rearrange("e a p n r -> p (e a) (n r)").bitcast(I32),
            )
            if e == 0:
                nc.sync.dma_start(out=bias[:], in_=b)
        nc.sync.dma_start(out=gates[:], in_=gate)
        nc.sync.dma_start(out=resid[:], in_=xr)

        def by_runs(raw, t0, t1):
            return raw[:, :, t0:t1].rearrange("p r (c i) -> p c r i", i=RUN)

        def interleaved(packed, t0, t1):
            return packed[:, t0:t1, :].rearrange("p (c i) r -> p c r i", i=RUN)

        def round_and_quantise(a, t0, width, by_vector):
            load0 = max(start for pass_, start in raws if pass_ == a and start <= t0)
            raw, c0 = raws[a, load0], t0 - load0
            packed = keep.tile([P, width, PACK], BF16, name=f"packed{a}_{t0}", align_bytes=64)
            nc.vector.tensor_copy(out=interleaved(packed, 0, by_vector), in_=by_runs(raw, c0, c0 + by_vector))
            nc.scalar.activation(
                interleaved(packed, by_vector, width), by_runs(raw, c0 + by_vector, c0 + width), Act.Copy
            )
            nc.vector.quantize_mx(
                out=token_codes[a][:, t0 : t0 + width].bitcast(FP8X4),
                scales=token_bytes[4 * a : P, t0 : t0 + width],
                in_=packed[:].rearrange("p t r -> p (t r)"),
            )

        def offsets_of(j0, slots):
            return offsets[:, j0 // OFFSETS_PER_COLUMN : (j0 + slots) // OFFSETS_PER_COLUMN]

        def gather(of_slots, of_tokens, j0, slots):
            nc.vector.tensor_copy(out=of_slots[:, j0 : j0 + slots], in_=of_tokens[:].indirect(offsets_of(j0, slots)))

        def expert(e):
            slots = slice(e * C, (e + 1) * C)
            acc = psum.tile([P, C], F32, name=f"acc{e}")
            for a in range(PASSES):
                nc.tensor.matmul_mx(
                    out=acc[:],
                    lhsT=w_codes[:, e * PASSES + a, :].bitcast(FP8X4),
                    lhsT_scale=w_bytes[:, e * PASSES + a, :],
                    rhs=slot_codes[a][:, slots].bitcast(FP8X4),
                    rhs_scale=slot_bytes[4 * a : P, slots],
                    start=(a == 0),
                    stop=(a == PASSES - 1),
                )
            nc.scalar.activation(relu[:, slots], acc[:], Act.Relu, bias=bias[:, e : e + 1])
            nc.scalar.activation(square[:, slots], relu[:, slots], Act.Square)

        for a in range(PASSES):
            t0 = 0
            for width, by_vector in CHUNKS[a]:
                round_and_quantise(a, t0, width, by_vector)
                t0 += width
            if a < PASSES - 1:
                gather(slot_codes[a], token_codes[a], 0, SLOTS)

        for (j0, slots), byte_gathers in LAST_GATHERS:
            gather(slot_codes[PASSES - 1], token_codes[PASSES - 1], j0, slots)
            for byte_j0, byte_slots in byte_gathers:
                gather(slot_bytes, token_bytes, byte_j0, byte_slots)
            for e in range(j0 // C, (j0 + slots) // C):
                expert(e)

        for j0, slots in SCATTERS:
            cols = slice(j0, j0 + slots)
            nc.vector.tensor_tensor(
                window[:].indirect(offsets_of(j0, slots)), square[:, cols], gates[:, cols], Alu.mult
            )
        for t0, width in STORES:
            cols = slice(t0, t0 + width)
            nc.vector.tensor_tensor(total[:, cols], window[:, cols], resid[:, cols], Alu.add)
            nc.sync.dma_start(out=out[:, cols], in_=total[:, cols])
